import numpy as np
import ml_dtypes


def mxq(x, axis, fmt="e4m3"):
    dtype, down = {"e4m3": (ml_dtypes.float8_e4m3fn, 7), "e5m2": (ml_dtypes.float8_e5m2, 14)}[fmt]
    v = np.moveaxis(np.asarray(x, np.float32).astype(ml_dtypes.bfloat16).astype(np.float64), axis, -1)
    blocks = v.reshape(v.shape[:-1] + (-1, 32))
    amax = np.abs(blocks).max(-1, keepdims=True)
    byte = np.maximum(np.where(amax > 0, np.frexp(amax)[1] - 1 + 127, 0) - down, 1)
    scale = np.exp2(byte - 127.0)
    codes = (blocks / scale).astype(np.float32).astype(dtype).astype(np.float64)
    return np.moveaxis((codes * scale).reshape(v.shape), -1, axis)


WIDE = False


def mx_kscale(k):
    if not WIDE:
        return np.ones(k)
    levels = np.array([10, -10, 5, -5, 0])
    if k % 512:
        return np.exp2(np.random.permutation(np.resize(levels, k // 32))).repeat(32)
    a = np.empty((k // 512, 16))
    for p in range(k // 512):
        a[p, :8] = np.random.permutation(np.resize(levels, 8))
        for g in range(8):
            far = levels[np.abs(levels - a[p, g]) >= 10]
            a[p, g + 8] = far[np.random.randint(len(far))]
    return np.exp2(a.ravel()).repeat(32)


def f64(x):
    return np.asarray(x).astype(np.float64)


def striped(idx):
    return np.tile(idx.reshape(-1, 16).T, (8, 1)).astype(np.uint16)


def unstriped(offs):
    return offs[:16].T.reshape(-1).astype(np.int64)


def striped8(idx):
    return np.concatenate([x.reshape(-1, 16).T for x in idx]).astype(np.uint16)


def runs(offs, k):
    lists = np.stack([offs[16 * r : 16 * r + 16].T.reshape(-1) for r in range(8)]).astype(np.int64)
    return lists[np.arange(k) % 512 // 64]


def pack_weight(w):
    k, n = w.shape
    w = f64(np.asarray(w, np.float32).astype(ml_dtypes.bfloat16)).reshape(k // 32, 32, n)
    amax = np.abs(w).max(1)
    byte = np.clip(np.where(amax > 0, np.frexp(amax)[1] - 1 + 127 - 7, 1), 1, 254)
    scaled = (w * np.exp2(127.0 - byte)[:, None, :]).reshape(k, n).astype(np.float32)
    words = np.ascontiguousarray(scaled.reshape(k // 512, 128, 4, n).transpose(0, 1, 3, 2)).astype(ml_dtypes.float8_e4m3fn).view(np.uint8)
    return words, np.ascontiguousarray(byte.astype(np.uint8).reshape(k // 512, 16, n))


def unpack_weight(words, scales):
    g, p, n, _ = words.shape
    vals = np.ascontiguousarray(words).view(ml_dtypes.float8_e4m3fn).astype(np.float64) * np.repeat(np.exp2(scales.astype(np.float64) - 127.0), 8, axis=1)[..., None]
    return vals.transpose(0, 1, 3, 2).reshape(g * 512, n)


K, T, S, N, G, H, W = 512, 2048, 512, 512, 2048, 512, 256


def setup_inputs():
    n = np.random.standard_normal
    s = mx_kscale(K)[:, None]
    u = mx_kscale(S)
    packed_xT = pack_weight(n((K, T)) * s)
    packed_dT = pack_weight(n((K, G)) / s)
    perm = np.stack([np.random.permutation(S) for _ in range(8)])
    return {
        "x_words": packed_xT[0],
        "x_scales": packed_xT[1],
        "d_words": packed_dT[0],
        "d_scales": packed_dT[1],
        "gn": (np.random.uniform(0.5, 1.5, (H, 1)) * u[:, None]).astype(np.float32),
        "w1": (n((H, N)) / np.sqrt(H) / u[:, None]).astype(np.float32),
        "offs": striped(np.random.permutation(T)[:S]),
        "k1": striped8(np.random.randint(0, G, (8, H))),
        "n1": striped8(np.stack([np.random.permutation(S) for _ in range(8)])),
        "n2": striped8(np.stack([np.random.permutation(S) for _ in range(8)])),
        "n3": striped8(perm[:, :W]),
        "n4": striped8(perm[:, W:]),
    }


def reference(x_words, x_scales, d_words, d_scales, gn, w1, offs, k1, n1, n2, n3, n4):
    d_k1 = unpack_weight(d_words, d_scales)[np.arange(K)[:, None], runs(k1, K)]
    xq = unpack_weight(x_words, x_scales)[:, unstriped(offs)]
    h = 0.0625 * (d_k1.T @ xq)
    ex = np.exp(h)
    z = f64(gn) * (np.log(ex + ex[np.arange(H)[:, None], runs(n1, H)]) - (h[np.arange(H)[:, None], runs(n2, H)]))
    h2 = mxq(f64(w1), 0, "e4m3").T @ mxq(z, 0, "e4m3")
    pa = h2[np.arange(N)[:, None], runs(n3, N)]
    pb = h2[np.arange(N)[:, None], runs(n4, N)]
    ra = np.maximum(pa, pb)
    out = h2.copy()
    out[np.arange(N)[:, None], runs(n3, N)] = ra
    return out

@@ -1,0 +1,191 @@
+from contextlib import ExitStack
+
+import concourse.mybir as mybir
+
+F32 = mybir.dt.float32
+BF16 = mybir.dt.bfloat16
+I32 = mybir.dt.int32
+U32 = mybir.dt.uint32
+U16 = mybir.dt.uint16
+U8 = mybir.dt.uint8
+FP8X4 = mybir.dt.float8_e4m3fn_x4
+ALU = mybir.AluOpType
+ACT = mybir.ActivationFunctionType
+
+P = 128
+PACK = 4
+TABLE = 2048
+S = 512
+HALF = S // 2
+PAIRS = 256
+W_EARLY = 128
+FLOPS = 2 * 2 * 512 * 512 * 512
+
+
+def tile_picked_pqlaylsefill_none_p_kernel(
+    tc, x_words, x_scales, d_words, d_scales, gn, w1, offs, k1, n1, n2, n3, n4, out
+):
+    nc = tc.nc
+    with ExitStack() as ctx:
+        lists = ctx.enter_context(tc.tile_pool(name="lists", bufs=1))
+        keep = ctx.enter_context(tc.tile_pool(name="keep", bufs=1))
+        work = ctx.enter_context(tc.tile_pool(name="work", bufs=4))
+        psum = ctx.enter_context(tc.psum_pool(name="psum", bufs=8))
+
+        def load_list(src, name):
+            t = lists.tile([P, src.shape[1]], U16, name=name)
+            nc.sync.dma_start(t[:], src)
+            return t
+
+        d_byte_table = keep.tile([P, TABLE], U8, name="d_byte_table", align_bytes=64)
+        x_byte_table = keep.tile([P, TABLE], U8, name="x_byte_table", align_bytes=64)
+        nc.vector.memset(d_byte_table[:].bitcast(I32), 0)
+        nc.vector.memset(x_byte_table[:].bitcast(I32), 0)
+
+        nc.sync.dma_start(d_byte_table[0:P:8, :].bitcast(I32), d_scales[0].bitcast(I32))
+        nc.sync.dma_start(x_byte_table[0:P:8, :].bitcast(I32), x_scales[0].bitcast(I32))
+        k1_t = load_list(k1, "k1_t")
+        offs_t = load_list(offs, "offs_t")
+        n1_t = load_list(n1, "n1_t")
+        n2_t = load_list(n2, "n2_t")
+        n3_t = load_list(n3, "n3_t")
+        n4_t = load_list(n4, "n4_t")
+        gain = keep.tile([P, PACK], F32, name="gain")
+        nc.sync.dma_start(gain[:], gn.rearrange("(p t) o -> p (t o)", t=PACK))
+        w_rows = w1.rearrange("(p j) c -> p j c", j=PACK)
+        w_early = keep.tile([P, PACK, W_EARLY], F32, name="w_early")
+        nc.sync.dma_start(w_early[:], w_rows[:, :, 0:W_EARLY])
+        d_word_table = keep.tile([P, TABLE], U32, name="d_word_table", align_bytes=64)
+        x_word_table = keep.tile([P, TABLE], U32, name="x_word_table", align_bytes=64)
+        nc.sync.dma_start(d_word_table[:].bitcast(I32), d_words[0].rearrange("p n t -> p (n t)").bitcast(I32))
+        nc.sync.dma_start(x_word_table[:].bitcast(I32), x_words[0].rearrange("p n t -> p (n t)").bitcast(I32))
+        w_late = keep.tile([P, PACK, S - W_EARLY], F32, name="w_late")
+        nc.sync.dma_start(w_late[:], w_rows[:, :, W_EARLY:S])
+
+        w_bf = keep.tile([P, PACK * S], BF16, name="w_bf", align_bytes=64)
+        w_view = w_bf[:].rearrange("p (t m j) -> p m j t", t=PACK, j=PACK)
+        nc.scalar.copy(w_view[:, 0 : W_EARLY // PACK, :, :], w_early[:].rearrange("p j (m t) -> p m j t", t=PACK))
+
+        d_bytes = keep.tile([P, S], U8, name="d_bytes", align_bytes=64)
+        x_bytes = keep.tile([P, S], U8, name="x_bytes", align_bytes=64)
+        spread = keep.tile([P, 2 * S], U8, name="spread", align_bytes=64)
+        planes = keep.tile([P, 2 * S], U8, name="planes", align_bytes=64)
+        nc.vector.tensor_copy(d_bytes[:], d_byte_table[:].indirect(k1_t[:]))
+        nc.vector.tensor_copy(x_bytes[:], x_byte_table[:].indirect(offs_t[:]))
+        nc.vector.tensor_copy(
+            spread[:, 0:S].rearrange("p (t m) -> p m t", t=PACK),
+            d_bytes[:].rearrange("p (m t) -> p m t", t=PACK),
+        )
+        nc.vector.tensor_copy(spread[:, S : 2 * S].bitcast(I32), x_bytes[:].bitcast(I32))
+        nc.vector.tensor_copy(planes[:].bitcast(I32), spread[:].bitcast(I32))
+        for r in range(1, 4):
+            nc.scalar.dma_start(planes[r:P:32, :].bitcast(I32), spread[8 * r : P : 32, :].bitcast(I32))
+
+        d_picked = keep.tile([P, S], U32, name="d_picked", align_bytes=64)
+        d_codes = keep.tile([P, S], U32, name="d_codes", align_bytes=64)
+        x_codes = keep.tile([P, S], U32, name="x_codes", align_bytes=64)
+        nc.vector.tensor_copy(d_picked[:], d_word_table[:].indirect(k1_t[:]))
+        nc.vector.tensor_copy(
+            d_codes[:].bitcast(I32).rearrange("p (t m) -> p m t", t=PACK),
+            d_picked[:].bitcast(I32).rearrange("p (m t) -> p m t", t=PACK),
+        )
+        nc.vector.tensor_copy(x_codes[:], x_word_table[:].indirect(offs_t[:]))
+
+        ex, ex_plain, em = [], [], []
+        for t in range(PACK):
+            cols = slice(t * P, (t + 1) * P)
+            acc = psum.tile([P, S], F32, name="acc")
+            nc.tensor.matmul_mx(
+                out=acc[:],
+                lhsT=d_codes[:, cols].bitcast(FP8X4),
+                lhsT_scale=planes[:, cols],
+                rhs=x_codes[:].bitcast(FP8X4),
+                rhs_scale=planes[:, S : 2 * S],
+                start=True,
+                stop=True,
+            )
+            a = work.tile([P, S], F32, name="ex")
+            b = work.tile([P, S], F32, name="ex_plain")
+            c = work.tile([P, S], F32, name="em")
+            nc.scalar.activation(a[:], acc[:], ACT.Exp, scale=0.0625)
+            nc.scalar.activation(b[:], acc[:], ACT.Exp, scale=0.0625)
+            nc.scalar.activation(c[:], acc[:], ACT.Exp, scale=-0.0625)
+            ex.append(a)
+            ex_plain.append(b)
+            em.append(c)
+
+        nc.vector.tensor_copy(w_view[:, W_EARLY // PACK : P, :, :], w_late[:].rearrange("p j (m t) -> p m j t", t=PACK))
+        w_codes = keep.tile([P, S], U32, name="w_codes", align_bytes=64)
+        w_scales = keep.tile([P, S], U8, name="w_scales", align_bytes=64)
+        nc.vector.quantize_mx(out=w_codes[:].bitcast(FP8X4), scales=w_scales[:], in_=w_bf[:])
+
+        ratio = [keep.tile([P, PACK, HALF], F32, name=f"ratio{u}") for u in range(2)]
+        sums = {}
+
+        def add_partner(t, u):
+            s = work.tile([P, HALF], F32, name="pair_sum")
+            nc.vector.tensor_tensor(
+                s[:], ex[t][:].indirect(n1_t[:, u * 16 : (u + 1) * 16]), ex_plain[t][:, u * HALF : (u + 1) * HALF], ALU.add
+            )
+            sums[(t, u)] = s
+
+        def divide(t, u):
+            nc.vector.tensor_tensor(
+                ratio[u][:, t, :], em[t][:].indirect(n2_t[:, u * 16 : (u + 1) * 16]), sums[(t, u)][:], ALU.mult
+            )
+
+        for steps in ([(0, 0), (0, 1)], [(1, 0), (1, 1)], [(2, 0), (3, 0)], [(2, 1), (3, 1)]):
+            for t, u in steps:
+                add_partner(t, u)
+            for t, u in steps:
+                divide(t, u)
+
+        z_bf = []
+        for u in range(2):
+            logs = keep.tile([P, HALF * PACK], F32, name=f"logs{u}")
+            nc.scalar.activation(
+                logs[:].rearrange("p (c i t) -> p c t i", i=4, t=PACK),
+                ratio[u][:].rearrange("p t (c i) -> p c t i", i=4),
+                ACT.Ln,
+            )
+            zb = keep.tile([P, HALF * PACK], BF16, name=f"z_bf{u}", align_bytes=64)
+            nc.vector.tensor_tensor(
+                zb[:].rearrange("p (j t) -> p j t", t=PACK),
+                logs[:].rearrange("p (j t) -> p j t", t=PACK),
+                gain[:].unsqueeze(1).to_broadcast([P, HALF, PACK]),
+                ALU.mult,
+            )
+            z_bf.append(zb)
+
+        h2 = [keep.tile([P, S], F32, name=f"h2_{t}") for t in range(PACK)]
+        for u in range(2):
+            z_codes = keep.tile([P, HALF], U32, name=f"z_codes{u}", align_bytes=64)
+            z_scales = keep.tile([P, HALF], U8, name=f"z_scales{u}", align_bytes=64)
+            nc.vector.quantize_mx(out=z_codes[:].bitcast(FP8X4), scales=z_scales[:], in_=z_bf[u][:])
+            for t in range(PACK):
+                cols = slice(t * P, (t + 1) * P)
+                acc = psum.tile([P, S], F32, name="acc")
+                nc.tensor.matmul_mx(
+                    out=acc[:, 0:HALF],
+                    lhsT=w_codes[:, cols].bitcast(FP8X4),
+                    lhsT_scale=w_scales[:, cols],
+                    rhs=z_codes[:].bitcast(FP8X4),
+                    rhs_scale=z_scales[:],
+                    start=True,
+                    stop=True,
+                )
+                nc.scalar.copy(h2[t][:, u * HALF : (u + 1) * HALF], acc[:, 0:HALF])
+
+        out_rows = out.rearrange("(p t) c -> t p c", t=PACK)
+        for t in range(PACK):
+            pa = work.tile([P, PAIRS], F32, name="pa")
+            pb = work.tile([P, PAIRS], F32, name="pb")
+            ra = work.tile([P, PAIRS], F32, name="ra")
+            nc.scalar.activation(pa[:], h2[t][:].indirect(n3_t[:]), ACT.Copy)
+            if t == 0:
+                nc.vector.tensor_copy(pb[:], h2[t][:].indirect(n4_t[:]))
+            else:
+                nc.scalar.activation(pb[:], h2[t][:].indirect(n4_t[:]), ACT.Copy)
+            nc.vector.tensor_tensor(ra[:], pa[:], pb[:], ALU.max)
+            nc.vector.tensor_copy(h2[t][:].indirect(n3_t[:]), ra[:])
+            nc.sync.dma_start(out_rows[t], h2[t][:])

@@ -18,7 +18,6 @@ TABLE = 2048
 S = 512
 HALF = S // 2
 PAIRS = 256
-W_EARLY = 128
 FLOPS = 2 * 2 * 512 * 512 * 512
 
 
@@ -38,50 +37,46 @@ def tile_picked_pqlaylsefill_none_p_kernel(
             return t
 
         d_byte_table = keep.tile([P, TABLE], U8, name="d_byte_table", align_bytes=64)
-        x_byte_table = keep.tile([P, TABLE], U8, name="x_byte_table", align_bytes=64)
+        x_byte_table = keep.tile([P, TABLE], U8, name="x_byte_table", tag="reused", align_bytes=64)
+        planes = keep.tile([P, 2 * S], U8, name="planes", align_bytes=64)
         nc.vector.memset(d_byte_table[:].bitcast(I32), 0)
         nc.vector.memset(x_byte_table[:].bitcast(I32), 0)
 
         nc.sync.dma_start(d_byte_table[0:P:8, :].bitcast(I32), d_scales[0].bitcast(I32))
         nc.sync.dma_start(x_byte_table[0:P:8, :].bitcast(I32), x_scales[0].bitcast(I32))
+        d_word_table = keep.tile([P, TABLE], U32, name="d_word_table", align_bytes=64)
+        x_word_table = keep.tile([P, TABLE], U32, name="x_word_table", align_bytes=64)
+        nc.sync.dma_start(d_word_table[:].bitcast(I32), d_words[0].rearrange("p n t -> p (n t)").bitcast(I32))
         k1_t = load_list(k1, "k1_t")
         offs_t = load_list(offs, "offs_t")
         n1_t = load_list(n1, "n1_t")
         n2_t = load_list(n2, "n2_t")
+        nc.sync.dma_start(x_word_table[:].bitcast(I32), x_words[0].rearrange("p n t -> p (n t)").bitcast(I32))
+        w_rows = w1.rearrange("(p j) c -> p j c", j=PACK)
+        w_bf = keep.tile([P, PACK * S], BF16, name="w_bf", align_bytes=64)
+        w_view = w_bf[:].rearrange("p (t m j) -> p m j t", t=PACK, j=PACK)
+        for u in range(2):
+            w_raw = keep.tile([P, PACK, HALF], F32, name=f"w_raw{u}")
+            nc.sync.dma_start(w_raw[:], w_rows[:, :, u * HALF : (u + 1) * HALF])
+            nc.scalar.copy(w_view[:, u * 64 : (u + 1) * 64, :, :], w_raw[:].rearrange("p j (m t) -> p m j t", t=PACK))
         n3_t = load_list(n3, "n3_t")
         n4_t = load_list(n4, "n4_t")
         gain = keep.tile([P, PACK], F32, name="gain")
         nc.sync.dma_start(gain[:], gn.rearrange("(p t) o -> p (t o)", t=PACK))
-        w_rows = w1.rearrange("(p j) c -> p j c", j=PACK)
-        w_early = keep.tile([P, PACK, W_EARLY], F32, name="w_early")
-        nc.sync.dma_start(w_early[:], w_rows[:, :, 0:W_EARLY])
-        d_word_table = keep.tile([P, TABLE], U32, name="d_word_table", align_bytes=64)
-        x_word_table = keep.tile([P, TABLE], U32, name="x_word_table", align_bytes=64)
-        nc.sync.dma_start(d_word_table[:].bitcast(I32), d_words[0].rearrange("p n t -> p (n t)").bitcast(I32))
-        nc.sync.dma_start(x_word_table[:].bitcast(I32), x_words[0].rearrange("p n t -> p (n t)").bitcast(I32))
-        w_late = keep.tile([P, PACK, S - W_EARLY], F32, name="w_late")
-        nc.sync.dma_start(w_late[:], w_rows[:, :, W_EARLY:S])
-
-        w_bf = keep.tile([P, PACK * S], BF16, name="w_bf", align_bytes=64)
-        w_view = w_bf[:].rearrange("p (t m j) -> p m j t", t=PACK, j=PACK)
-        nc.scalar.copy(w_view[:, 0 : W_EARLY // PACK, :, :], w_early[:].rearrange("p j (m t) -> p m j t", t=PACK))
 
         d_bytes = keep.tile([P, S], U8, name="d_bytes", align_bytes=64)
         x_bytes = keep.tile([P, S], U8, name="x_bytes", align_bytes=64)
-        spread = keep.tile([P, 2 * S], U8, name="spread", align_bytes=64)
-        planes = keep.tile([P, 2 * S], U8, name="planes", align_bytes=64)
         nc.vector.tensor_copy(d_bytes[:], d_byte_table[:].indirect(k1_t[:]))
         nc.vector.tensor_copy(x_bytes[:], x_byte_table[:].indirect(offs_t[:]))
         nc.vector.tensor_copy(
-            spread[:, 0:S].rearrange("p (t m) -> p m t", t=PACK),
+            planes[:, 0:S].rearrange("p (t m) -> p m t", t=PACK),
             d_bytes[:].rearrange("p (m t) -> p m t", t=PACK),
         )
-        nc.vector.tensor_copy(spread[:, S : 2 * S].bitcast(I32), x_bytes[:].bitcast(I32))
-        nc.vector.tensor_copy(planes[:].bitcast(I32), spread[:].bitcast(I32))
-        for r in range(1, 4):
-            nc.scalar.dma_start(planes[r:P:32, :].bitcast(I32), spread[8 * r : P : 32, :].bitcast(I32))
+        nc.vector.tensor_copy(planes[:, S : 2 * S].bitcast(I32), x_bytes[:].bitcast(I32))
+        for r, queue in ((1, nc.sync), (2, nc.scalar), (3, nc.sync)):
+            queue.dma_start(planes[r:P:32, :].bitcast(I32), planes[8 * r : P : 32, :].bitcast(I32))
 
-        d_picked = keep.tile([P, S], U32, name="d_picked", align_bytes=64)
+        d_picked = keep.tile([P, S], U32, name="d_picked", tag="reused", align_bytes=64)
         d_codes = keep.tile([P, S], U32, name="d_codes", align_bytes=64)
         x_codes = keep.tile([P, S], U32, name="x_codes", align_bytes=64)
         nc.vector.tensor_copy(d_picked[:], d_word_table[:].indirect(k1_t[:]))
@@ -89,58 +84,94 @@ def tile_picked_pqlaylsefill_none_p_kernel(
             d_codes[:].bitcast(I32).rearrange("p (t m) -> p m t", t=PACK),
             d_picked[:].bitcast(I32).rearrange("p (m t) -> p m t", t=PACK),
         )
-        nc.vector.tensor_copy(x_codes[:], x_word_table[:].indirect(offs_t[:]))
 
-        ex, ex_plain, em = [], [], []
-        for t in range(PACK):
+        def half(u):
+            return slice(u * HALF, (u + 1) * HALF)
+
+        def list_half(u):
+            return slice(u * HALF // 16, (u + 1) * HALF // 16)
+
+        for u in range(2):
+            nc.vector.tensor_copy(x_codes[:, half(u)], x_word_table[:].indirect(offs_t[:, list_half(u)]))
+
+        def first_product(t, lo, hi):
             cols = slice(t * P, (t + 1) * P)
             acc = psum.tile([P, S], F32, name="acc")
             nc.tensor.matmul_mx(
-                out=acc[:],
+                out=acc[:, 0 : hi - lo],
                 lhsT=d_codes[:, cols].bitcast(FP8X4),
                 lhsT_scale=planes[:, cols],
-                rhs=x_codes[:].bitcast(FP8X4),
-                rhs_scale=planes[:, S : 2 * S],
+                rhs=x_codes[:, lo:hi].bitcast(FP8X4),
+                rhs_scale=planes[:, S + lo : S + hi],
                 start=True,
                 stop=True,
             )
-            a = work.tile([P, S], F32, name="ex")
-            b = work.tile([P, S], F32, name="ex_plain")
-            c = work.tile([P, S], F32, name="em")
-            nc.scalar.activation(a[:], acc[:], ACT.Exp, scale=0.0625)
-            nc.scalar.activation(b[:], acc[:], ACT.Exp, scale=0.0625)
-            nc.scalar.activation(c[:], acc[:], ACT.Exp, scale=-0.0625)
-            ex.append(a)
-            ex_plain.append(b)
-            em.append(c)
+            return acc[:, 0 : hi - lo]
 
-        nc.vector.tensor_copy(w_view[:, W_EARLY // PACK : P, :, :], w_late[:].rearrange("p j (m t) -> p m j t", t=PACK))
+        h0_halves = [first_product(0, u * HALF, (u + 1) * HALF) for u in range(2)]
+        h_acc = {t: first_product(t, 0, S) for t in range(1, PACK)}
+
         w_codes = keep.tile([P, S], U32, name="w_codes", align_bytes=64)
         w_scales = keep.tile([P, S], U8, name="w_scales", align_bytes=64)
         nc.vector.quantize_mx(out=w_codes[:].bitcast(FP8X4), scales=w_scales[:], in_=w_bf[:])
 
+        ex = [keep.tile([P, S], F32, name=f"ex{t}") for t in range(PACK)]
+        em = [keep.tile([P, S], F32, name=f"em{t}") for t in range(PACK)]
+        other = [[keep.tile([P, HALF], F32, name=f"other{t}_{u}") for u in range(2)] for t in range(PACK)]
+        sums = [[keep.tile([P, HALF], F32, name=f"sum{t}_{u}") for u in range(2)] for t in range(PACK)]
         ratio = [keep.tile([P, PACK, HALF], F32, name=f"ratio{u}") for u in range(2)]
-        sums = {}
+        LAST = PACK - 1
+
+        def make_ex(t):
+            nc.scalar.activation(ex[t][:], h_acc[t], ACT.Exp, scale=0.0625)
+
+        def make_em(t):
+            nc.scalar.activation(em[t][:], h_acc[t], ACT.Exp, scale=-0.0625)
+
+        def make_other(t, u):
+            if t == LAST:
+                nc.scalar.activation(other[t][u][:], ex[t][:].indirect(n1_t[:, list_half(u)]), ACT.Copy)
+            else:
+                nc.scalar.activation(other[t][u][:], h_acc[t][:, half(u)], ACT.Exp, scale=0.0625)
 
         def add_partner(t, u):
-            s = work.tile([P, HALF], F32, name="pair_sum")
-            nc.vector.tensor_tensor(
-                s[:], ex[t][:].indirect(n1_t[:, u * 16 : (u + 1) * 16]), ex_plain[t][:, u * HALF : (u + 1) * HALF], ALU.add
-            )
-            sums[(t, u)] = s
+            if t == LAST:
+                nc.vector.tensor_tensor(sums[t][u][:], other[t][u][:], ex[t][:, half(u)], ALU.add)
+            else:
+                nc.vector.tensor_tensor(sums[t][u][:], ex[t][:].indirect(n1_t[:, list_half(u)]), other[t][u][:], ALU.add)
 
         def divide(t, u):
-            nc.vector.tensor_tensor(
-                ratio[u][:, t, :], em[t][:].indirect(n2_t[:, u * 16 : (u + 1) * 16]), sums[(t, u)][:], ALU.mult
-            )
+            nc.vector.tensor_tensor(ratio[u][:, t, :], em[t][:].indirect(n2_t[:, list_half(u)]), sums[t][u][:], ALU.mult)
 
-        for steps in ([(0, 0), (0, 1)], [(1, 0), (1, 1)], [(2, 0), (3, 0)], [(2, 1), (3, 1)]):
-            for t, u in steps:
+        for u in range(2):
+            nc.scalar.activation(ex[0][:, half(u)], h0_halves[u], ACT.Exp, scale=0.0625)
+            nc.scalar.activation(other[0][u][:], h0_halves[u], ACT.Exp, scale=0.0625)
+        for u in range(2):
+            nc.scalar.activation(em[0][:, half(u)], h0_halves[u], ACT.Exp, scale=-0.0625)
+        make_ex(1)
+        for u in range(2):
+            make_other(1, u)
+        make_em(1)
+        for t in (0, 1):
+            for u in range(2):
                 add_partner(t, u)
-            for t, u in steps:
+            for u in range(2):
+                divide(t, u)
+        for t in (2, 3):
+            make_ex(t)
+            make_other(t, 0)
+        for t in (2, 3):
+            make_em(t)
+        for t in (2, 3):
+            make_other(t, 1)
+        for u in range(2):
+            for t in (2, 3):
+                add_partner(t, u)
+            for t in (2, 3):
                 divide(t, u)
 
-        z_bf = []
+        h2 = [keep.tile([P, S], F32, name=f"h2_{t}") for t in range(PACK)]
+        h2_acc = {}
         for u in range(2):
             logs = keep.tile([P, HALF * PACK], F32, name=f"logs{u}")
             nc.scalar.activation(
@@ -148,20 +179,16 @@ def tile_picked_pqlaylsefill_none_p_kernel(
                 ratio[u][:].rearrange("p t (c i) -> p c t i", i=4),
                 ACT.Ln,
             )
-            zb = keep.tile([P, HALF * PACK], BF16, name=f"z_bf{u}", align_bytes=64)
+            z_bf = keep.tile([P, HALF * PACK], BF16, name="z_bf", align_bytes=64)
             nc.vector.tensor_tensor(
-                zb[:].rearrange("p (j t) -> p j t", t=PACK),
+                z_bf[:].rearrange("p (j t) -> p j t", t=PACK),
                 logs[:].rearrange("p (j t) -> p j t", t=PACK),
                 gain[:].unsqueeze(1).to_broadcast([P, HALF, PACK]),
                 ALU.mult,
             )
-            z_bf.append(zb)
-
-        h2 = [keep.tile([P, S], F32, name=f"h2_{t}") for t in range(PACK)]
-        for u in range(2):
             z_codes = keep.tile([P, HALF], U32, name=f"z_codes{u}", align_bytes=64)
             z_scales = keep.tile([P, HALF], U8, name=f"z_scales{u}", align_bytes=64)
-            nc.vector.quantize_mx(out=z_codes[:].bitcast(FP8X4), scales=z_scales[:], in_=z_bf[u][:])
+            nc.vector.quantize_mx(out=z_codes[:].bitcast(FP8X4), scales=z_scales[:], in_=z_bf[:])
             for t in range(PACK):
                 cols = slice(t * P, (t + 1) * P)
                 acc = psum.tile([P, S], F32, name="acc")
@@ -174,10 +201,13 @@ def tile_picked_pqlaylsefill_none_p_kernel(
                     start=True,
                     stop=True,
                 )
-                nc.scalar.copy(h2[t][:, u * HALF : (u + 1) * HALF], acc[:, 0:HALF])
+                h2_acc[(t, u)] = acc
+        for t in range(PACK):
+            nc.scalar.copy(h2[t][:, half(0)], h2_acc[(t, 0)][:, 0:HALF])
 
         out_rows = out.rearrange("(p t) c -> t p c", t=PACK)
         for t in range(PACK):
+            nc.scalar.copy(h2[t][:, half(1)], h2_acc[(t, 1)][:, 0:HALF])
             pa = work.tile([P, PAIRS], F32, name="pa")
             pb = work.tile([P, PAIRS], F32, name="pb")
             ra = work.tile([P, PAIRS], F32, name="ra")

@@ -18,6 +18,7 @@ TABLE = 2048
 S = 512
 HALF = S // 2
 PAIRS = 256
+W_EARLY = 384
 FLOPS = 2 * 2 * 512 * 512 * 512
 
 
@@ -28,6 +29,7 @@ def tile_picked_pqlaylsefill_none_p_kernel(
     with ExitStack() as ctx:
         lists = ctx.enter_context(tc.tile_pool(name="lists", bufs=1))
         keep = ctx.enter_context(tc.tile_pool(name="keep", bufs=1))
+        shared = ctx.enter_context(tc.tile_pool(name="shared", bufs=1))
         work = ctx.enter_context(tc.tile_pool(name="work", bufs=4))
         psum = ctx.enter_context(tc.psum_pool(name="psum", bufs=8))
 
@@ -46,35 +48,38 @@ def tile_picked_pqlaylsefill_none_p_kernel(
         nc.sync.dma_start(x_byte_table[0:P:8, :].bitcast(I32), x_scales[0].bitcast(I32))
         d_word_table = keep.tile([P, TABLE], U32, name="d_word_table", align_bytes=64)
         x_word_table = keep.tile([P, TABLE], U32, name="x_word_table", align_bytes=64)
-        nc.sync.dma_start(d_word_table[:].bitcast(I32), d_words[0].rearrange("p n t -> p (n t)").bitcast(I32))
+        d_word_rows = d_words[0].rearrange("p n t -> p (n t)").bitcast(I32)
+        nc.sync.dma_start(d_word_table[:].bitcast(I32)[:, 0 : TABLE // 2], d_word_rows[:, 0 : TABLE // 2])
         k1_t = load_list(k1, "k1_t")
         offs_t = load_list(offs, "offs_t")
         n1_t = load_list(n1, "n1_t")
         n2_t = load_list(n2, "n2_t")
-        nc.sync.dma_start(x_word_table[:].bitcast(I32), x_words[0].rearrange("p n t -> p (n t)").bitcast(I32))
+        nc.sync.dma_start(d_word_table[:].bitcast(I32)[:, TABLE // 2 : TABLE], d_word_rows[:, TABLE // 2 : TABLE])
         w_rows = w1.rearrange("(p j) c -> p j c", j=PACK)
         w_bf = keep.tile([P, PACK * S], BF16, name="w_bf", align_bytes=64)
-        w_view = w_bf[:].rearrange("p (t m j) -> p m j t", t=PACK, j=PACK)
-        for u in range(2):
-            w_raw = keep.tile([P, PACK, HALF], F32, name=f"w_raw{u}")
-            nc.sync.dma_start(w_raw[:], w_rows[:, :, u * HALF : (u + 1) * HALF])
-            nc.scalar.copy(w_view[:, u * 64 : (u + 1) * 64, :, :], w_raw[:].rearrange("p j (m t) -> p m j t", t=PACK))
+        w_view = w_bf[:].rearrange("p (t m j) -> p m t j", t=PACK, j=PACK)
+        w_early = keep.tile([P, PACK, W_EARLY], F32, name="w_early")
+        nc.sync.dma_start(w_early[:], w_rows[:, :, 0:W_EARLY])
+        nc.scalar.copy(w_view[:, 0 : W_EARLY // PACK, :, :], w_early[:].rearrange("p j (m t) -> p m t j", t=PACK))
+        nc.sync.dma_start(x_word_table[:].bitcast(I32), x_words[0].rearrange("p n t -> p (n t)").bitcast(I32))
         n3_t = load_list(n3, "n3_t")
         n4_t = load_list(n4, "n4_t")
         gain = keep.tile([P, PACK], F32, name="gain")
         nc.sync.dma_start(gain[:], gn.rearrange("(p t) o -> p (t o)", t=PACK))
 
-        d_bytes = keep.tile([P, S], U8, name="d_bytes", align_bytes=64)
-        x_bytes = keep.tile([P, S], U8, name="x_bytes", align_bytes=64)
+        d_bytes = shared.tile([P, S], U8, name="d_bytes", align_bytes=64, offset=0)
+        x_bytes = shared.tile([P, S], U8, name="x_bytes", align_bytes=64, offset=S)
         nc.vector.tensor_copy(d_bytes[:], d_byte_table[:].indirect(k1_t[:]))
         nc.vector.tensor_copy(x_bytes[:], x_byte_table[:].indirect(offs_t[:]))
         nc.vector.tensor_copy(
-            planes[:, 0:S].rearrange("p (t m) -> p m t", t=PACK),
-            d_bytes[:].rearrange("p (m t) -> p m t", t=PACK),
+            planes[:, 0:S].rearrange("p (t m) -> p t m", t=PACK),
+            d_bytes[:].rearrange("p (m t) -> p t m", t=PACK),
         )
         nc.vector.tensor_copy(planes[:, S : 2 * S].bitcast(I32), x_bytes[:].bitcast(I32))
-        for r, queue in ((1, nc.sync), (2, nc.scalar), (3, nc.sync)):
-            queue.dma_start(planes[r:P:32, :].bitcast(I32), planes[8 * r : P : 32, :].bitcast(I32))
+        for r in range(1, 4):
+            nc.sync.dma_start(planes[r:P:32, :].bitcast(I32), planes[8 * r : P : 32, :].bitcast(I32))
+        w_late = shared.tile([P, PACK, S - W_EARLY], F32, name="w_late", align_bytes=64, offset=0)
+        nc.sync.dma_start(w_late[:], w_rows[:, :, W_EARLY:S])
 
         d_picked = keep.tile([P, S], U32, name="d_picked", tag="reused", align_bytes=64)
         d_codes = keep.tile([P, S], U32, name="d_codes", align_bytes=64)
@@ -111,6 +116,7 @@ def tile_picked_pqlaylsefill_none_p_kernel(
         h0_halves = [first_product(0, u * HALF, (u + 1) * HALF) for u in range(2)]
         h_acc = {t: first_product(t, 0, S) for t in range(1, PACK)}
 
+        nc.vector.tensor_copy(w_view[:, W_EARLY // PACK : P, :, :], w_late[:].rearrange("p j (m t) -> p m t j", t=PACK))
         w_codes = keep.tile([P, S], U32, name="w_codes", align_bytes=64)
         w_scales = keep.tile([P, S], U8, name="w_scales", align_bytes=64)
         nc.vector.quantize_mx(out=w_codes[:].bitcast(FP8X4), scales=w_scales[:], in_=w_bf[:])
@@ -206,16 +212,19 @@ def tile_picked_pqlaylsefill_none_p_kernel(
             nc.scalar.copy(h2[t][:, half(0)], h2_acc[(t, 0)][:, 0:HALF])
 
         out_rows = out.rearrange("(p t) c -> t p c", t=PACK)
-        for t in range(PACK):
-            nc.scalar.copy(h2[t][:, half(1)], h2_acc[(t, 1)][:, 0:HALF])
-            pa = work.tile([P, PAIRS], F32, name="pa")
-            pb = work.tile([P, PAIRS], F32, name="pb")
-            ra = work.tile([P, PAIRS], F32, name="ra")
-            nc.scalar.activation(pa[:], h2[t][:].indirect(n3_t[:]), ACT.Copy)
-            if t == 0:
-                nc.vector.tensor_copy(pb[:], h2[t][:].indirect(n4_t[:]))
-            else:
-                nc.scalar.activation(pb[:], h2[t][:].indirect(n4_t[:]), ACT.Copy)
+        for group in ((0,), (1,), (2, 3)):
+            name = "_".join(str(t) for t in group)
+            pa = keep.tile([P, len(group), PAIRS], F32, name="pa" + name)
+            pb = keep.tile([P, len(group), PAIRS], F32, name="pb" + name)
+            ra = keep.tile([P, len(group), PAIRS], F32, name="ra" + name)
+            for i, t in enumerate(group):
+                nc.scalar.copy(h2[t][:, half(1)], h2_acc[(t, 1)][:, 0:HALF])
+                nc.scalar.activation(pa[:, i, :], h2[t][:].indirect(n3_t[:]), ACT.Copy)
+                if t == 0:
+                    nc.vector.tensor_copy(pb[:, i, :], h2[t][:].indirect(n4_t[:]))
+                else:
+                    nc.scalar.activation(pb[:, i, :], h2[t][:].indirect(n4_t[:]), ACT.Copy)
             nc.vector.tensor_tensor(ra[:], pa[:], pb[:], ALU.max)
-            nc.vector.tensor_copy(h2[t][:].indirect(n3_t[:]), ra[:])
-            nc.sync.dma_start(out_rows[t], h2[t][:])
+            for i, t in enumerate(group):
+                nc.vector.tensor_copy(h2[t][:].indirect(n3_t[:]), ra[:, i, :])
+                nc.sync.dma_start(out_rows[t], h2[t][:])

@@ -18,6 +18,7 @@ TABLE = 2048
 S = 512
 HALF = S // 2
 PAIRS = 256
+D_FIRST = 1280
 W_EARLY = 384
 FLOPS = 2 * 2 * 512 * 512 * 512
 
@@ -46,15 +47,15 @@ def tile_picked_pqlaylsefill_none_p_kernel(
 
         nc.sync.dma_start(d_byte_table[0:P:8, :].bitcast(I32), d_scales[0].bitcast(I32))
         nc.sync.dma_start(x_byte_table[0:P:8, :].bitcast(I32), x_scales[0].bitcast(I32))
+        k1_t = load_list(k1, "k1_t")
         d_word_table = keep.tile([P, TABLE], U32, name="d_word_table", align_bytes=64)
         x_word_table = keep.tile([P, TABLE], U32, name="x_word_table", align_bytes=64)
         d_word_rows = d_words[0].rearrange("p n t -> p (n t)").bitcast(I32)
-        nc.sync.dma_start(d_word_table[:].bitcast(I32)[:, 0 : TABLE // 2], d_word_rows[:, 0 : TABLE // 2])
-        k1_t = load_list(k1, "k1_t")
+        nc.sync.dma_start(d_word_table[:].bitcast(I32)[:, 0 : D_FIRST], d_word_rows[:, 0 : D_FIRST])
         offs_t = load_list(offs, "offs_t")
         n1_t = load_list(n1, "n1_t")
         n2_t = load_list(n2, "n2_t")
-        nc.sync.dma_start(d_word_table[:].bitcast(I32)[:, TABLE // 2 : TABLE], d_word_rows[:, TABLE // 2 : TABLE])
+        nc.sync.dma_start(d_word_table[:].bitcast(I32)[:, D_FIRST : TABLE], d_word_rows[:, D_FIRST : TABLE])
         w_rows = w1.rearrange("(p j) c -> p j c", j=PACK)
         w_bf = keep.tile([P, PACK * S], BF16, name="w_bf", align_bytes=64)
         w_view = w_bf[:].rearrange("p (t m j) -> p m t j", t=PACK, j=PACK)
@@ -123,10 +124,11 @@ def tile_picked_pqlaylsefill_none_p_kernel(
 
         ex = [keep.tile([P, S], F32, name=f"ex{t}") for t in range(PACK)]
         em = [keep.tile([P, S], F32, name=f"em{t}") for t in range(PACK)]
-        other = [[keep.tile([P, HALF], F32, name=f"other{t}_{u}") for u in range(2)] for t in range(PACK)]
         sums = [[keep.tile([P, HALF], F32, name=f"sum{t}_{u}") for u in range(2)] for t in range(PACK)]
         ratio = [keep.tile([P, PACK, HALF], F32, name=f"ratio{u}") for u in range(2)]
         LAST = PACK - 1
+        other = [[keep.tile([P, HALF], F32, name=f"other{t}_{u}")[:] for u in range(2)] for t in range(LAST)]
+        other.append([ratio[u][:, LAST - 1, :] for u in range(2)])
 
         def make_ex(t):
             nc.scalar.activation(ex[t][:], h_acc[t], ACT.Exp, scale=0.0625)
@@ -136,22 +138,22 @@ def tile_picked_pqlaylsefill_none_p_kernel(
 
         def make_other(t, u):
             if t == LAST:
-                nc.scalar.activation(other[t][u][:], ex[t][:].indirect(n1_t[:, list_half(u)]), ACT.Copy)
+                nc.scalar.activation(other[t][u], ex[t][:].indirect(n1_t[:, list_half(u)]), ACT.Copy)
             else:
-                nc.scalar.activation(other[t][u][:], h_acc[t][:, half(u)], ACT.Exp, scale=0.0625)
+                nc.scalar.activation(other[t][u], h_acc[t][:, half(u)], ACT.Exp, scale=0.0625)
 
         def add_partner(t, u):
             if t == LAST:
-                nc.vector.tensor_tensor(sums[t][u][:], other[t][u][:], ex[t][:, half(u)], ALU.add)
+                nc.vector.tensor_tensor(sums[t][u][:], other[t][u], ex[t][:, half(u)], ALU.add)
             else:
-                nc.vector.tensor_tensor(sums[t][u][:], ex[t][:].indirect(n1_t[:, list_half(u)]), other[t][u][:], ALU.add)
+                nc.vector.tensor_tensor(sums[t][u][:], ex[t][:].indirect(n1_t[:, list_half(u)]), other[t][u], ALU.add)
 
         def divide(t, u):
             nc.vector.tensor_tensor(ratio[u][:, t, :], em[t][:].indirect(n2_t[:, list_half(u)]), sums[t][u][:], ALU.mult)
 
         for u in range(2):
             nc.scalar.activation(ex[0][:, half(u)], h0_halves[u], ACT.Exp, scale=0.0625)
-            nc.scalar.activation(other[0][u][:], h0_halves[u], ACT.Exp, scale=0.0625)
+            nc.scalar.activation(other[0][u], h0_halves[u], ACT.Exp, scale=0.0625)
         for u in range(2):
             nc.scalar.activation(em[0][:, half(u)], h0_halves[u], ACT.Exp, scale=-0.0625)
         make_ex(1)
@@ -178,23 +180,30 @@ def tile_picked_pqlaylsefill_none_p_kernel(
 
         h2 = [keep.tile([P, S], F32, name=f"h2_{t}") for t in range(PACK)]
         h2_acc = {}
-        for u in range(2):
-            logs = keep.tile([P, HALF * PACK], F32, name=f"logs{u}")
+        z_codes = [keep.tile([P, HALF], U32, name=f"z_codes{u}", align_bytes=64) for u in range(2)]
+        z_scales = [keep.tile([P, HALF], U8, name=f"z_scales{u}", align_bytes=64) for u in range(2)]
+        z_bf = {}
+
+        def make_z(u, lo, hi, tag):
+            logs = keep.tile([P, (hi - lo) * PACK], F32, name=f"logs{u}_{lo}")
             nc.scalar.activation(
                 logs[:].rearrange("p (c i t) -> p c t i", i=4, t=PACK),
-                ratio[u][:].rearrange("p t (c i) -> p c t i", i=4),
+                ratio[u][:, :, lo:hi].rearrange("p t (c i) -> p c t i", i=4),
                 ACT.Ln,
             )
-            z_bf = keep.tile([P, HALF * PACK], BF16, name="z_bf", align_bytes=64)
+            zb = keep.tile([P, (hi - lo) * PACK], BF16, name=f"z_bf{u}_{lo}", tag=tag, align_bytes=64)
             nc.vector.tensor_tensor(
-                z_bf[:].rearrange("p (j t) -> p j t", t=PACK),
+                zb[:].rearrange("p (j t) -> p j t", t=PACK),
                 logs[:].rearrange("p (j t) -> p j t", t=PACK),
-                gain[:].unsqueeze(1).to_broadcast([P, HALF, PACK]),
+                gain[:].unsqueeze(1).to_broadcast([P, hi - lo, PACK]),
                 ALU.mult,
             )
-            z_codes = keep.tile([P, HALF], U32, name=f"z_codes{u}", align_bytes=64)
-            z_scales = keep.tile([P, HALF], U8, name=f"z_scales{u}", align_bytes=64)
-            nc.vector.quantize_mx(out=z_codes[:].bitcast(FP8X4), scales=z_scales[:], in_=z_bf[:])
+            z_bf[(u, lo)] = zb
+
+        def quantise_z(u, lo, hi):
+            nc.vector.quantize_mx(out=z_codes[u][:, lo:hi].bitcast(FP8X4), scales=z_scales[u][:, lo:hi], in_=z_bf[(u, lo)][:])
+
+        def second_product(u):
             for t in range(PACK):
                 cols = slice(t * P, (t + 1) * P)
                 acc = psum.tile([P, S], F32, name="acc")
@@ -202,12 +211,22 @@ def tile_picked_pqlaylsefill_none_p_kernel(
                     out=acc[:, 0:HALF],
                     lhsT=w_codes[:, cols].bitcast(FP8X4),
                     lhsT_scale=w_scales[:, cols],
-                    rhs=z_codes[:].bitcast(FP8X4),
-                    rhs_scale=z_scales[:],
+                    rhs=z_codes[u][:].bitcast(FP8X4),
+                    rhs_scale=z_scales[u][:],
                     start=True,
                     stop=True,
                 )
                 h2_acc[(t, u)] = acc
+
+        Q = HALF // 2
+        make_z(0, 0, HALF, "z_wide")
+        make_z(1, 0, Q, "z_narrow")
+        quantise_z(0, 0, HALF)
+        second_product(0)
+        make_z(1, Q, HALF, "z_wide")
+        quantise_z(1, 0, Q)
+        quantise_z(1, Q, HALF)
+        second_product(1)
         for t in range(PACK):
             nc.scalar.copy(h2[t][:, half(0)], h2_acc[(t, 0)][:, 0:HALF])
 

from contextlib import ExitStack

import concourse.mybir as mybir

F32 = mybir.dt.float32
BF16 = mybir.dt.bfloat16
I32 = mybir.dt.int32
U32 = mybir.dt.uint32
U16 = mybir.dt.uint16
U8 = mybir.dt.uint8
FP8X4 = mybir.dt.float8_e4m3fn_x4
ALU = mybir.AluOpType
ACT = mybir.ActivationFunctionType

P = 128
PACK = 4
TABLE = 2048
S = 512
HALF = S // 2
PAIRS = 256
D_FIRST = 1280
W_EARLY = 384
FLOPS = 2 * 2 * 512 * 512 * 512


def tile_picked_pqlaylsefill_none_p_kernel(
    tc, x_words, x_scales, d_words, d_scales, gn, w1, offs, k1, n1, n2, n3, n4, out
):
    nc = tc.nc
    with ExitStack() as ctx:
        lists = ctx.enter_context(tc.tile_pool(name="lists", bufs=1))
        keep = ctx.enter_context(tc.tile_pool(name="keep", bufs=1))
        shared = ctx.enter_context(tc.tile_pool(name="shared", bufs=1))
        work = ctx.enter_context(tc.tile_pool(name="work", bufs=4))
        psum = ctx.enter_context(tc.psum_pool(name="psum", bufs=8))

        def load_list(src, name):
            t = lists.tile([P, src.shape[1]], U16, name=name)
            nc.sync.dma_start(t[:], src)
            return t

        d_byte_table = keep.tile([P, TABLE], U8, name="d_byte_table", align_bytes=64)
        x_byte_table = keep.tile([P, TABLE], U8, name="x_byte_table", tag="reused", align_bytes=64)
        planes = keep.tile([P, 2 * S], U8, name="planes", align_bytes=64)
        nc.vector.memset(d_byte_table[:].bitcast(I32), 0)
        nc.vector.memset(x_byte_table[:].bitcast(I32), 0)

        nc.sync.dma_start(d_byte_table[0:P:8, :].bitcast(I32), d_scales[0].bitcast(I32))
        nc.sync.dma_start(x_byte_table[0:P:8, :].bitcast(I32), x_scales[0].bitcast(I32))
        k1_t = load_list(k1, "k1_t")
        d_word_table = keep.tile([P, TABLE], U32, name="d_word_table", align_bytes=64)
        x_word_table = keep.tile([P, TABLE], U32, name="x_word_table", align_bytes=64)
        d_word_rows = d_words[0].rearrange("p n t -> p (n t)").bitcast(I32)
        nc.sync.dma_start(d_word_table[:].bitcast(I32)[:, 0 : D_FIRST], d_word_rows[:, 0 : D_FIRST])
        offs_t = load_list(offs, "offs_t")
        n1_t = load_list(n1, "n1_t")
        n2_t = load_list(n2, "n2_t")
        nc.sync.dma_start(d_word_table[:].bitcast(I32)[:, D_FIRST : TABLE], d_word_rows[:, D_FIRST : TABLE])
        w_rows = w1.rearrange("(p j) c -> p j c", j=PACK)
        w_bf = keep.tile([P, PACK * S], BF16, name="w_bf", align_bytes=64)
        w_view = w_bf[:].rearrange("p (t m j) -> p m t j", t=PACK, j=PACK)
        w_early = keep.tile([P, PACK, W_EARLY], F32, name="w_early")
        nc.sync.dma_start(w_early[:], w_rows[:, :, 0:W_EARLY])
        nc.scalar.copy(w_view[:, 0 : W_EARLY // PACK, :, :], w_early[:].rearrange("p j (m t) -> p m t j", t=PACK))
        nc.sync.dma_start(x_word_table[:].bitcast(I32), x_words[0].rearrange("p n t -> p (n t)").bitcast(I32))
        n3_t = load_list(n3, "n3_t")
        n4_t = load_list(n4, "n4_t")
        gain = keep.tile([P, PACK], F32, name="gain")
        nc.sync.dma_start(gain[:], gn.rearrange("(p t) o -> p (t o)", t=PACK))

        d_bytes = shared.tile([P, S], U8, name="d_bytes", align_bytes=64, offset=0)
        x_bytes = shared.tile([P, S], U8, name="x_bytes", align_bytes=64, offset=S)
        nc.vector.tensor_copy(d_bytes[:], d_byte_table[:].indirect(k1_t[:]))
        nc.vector.tensor_copy(x_bytes[:], x_byte_table[:].indirect(offs_t[:]))
        nc.vector.tensor_copy(
            planes[:, 0:S].rearrange("p (t m) -> p t m", t=PACK),
            d_bytes[:].rearrange("p (m t) -> p t m", t=PACK),
        )
        nc.vector.tensor_copy(planes[:, S : 2 * S].bitcast(I32), x_bytes[:].bitcast(I32))
        for r in range(1, 4):
            nc.sync.dma_start(planes[r:P:32, :].bitcast(I32), planes[8 * r : P : 32, :].bitcast(I32))
        w_late = shared.tile([P, PACK, S - W_EARLY], F32, name="w_late", align_bytes=64, offset=0)
        nc.sync.dma_start(w_late[:], w_rows[:, :, W_EARLY:S])

        d_picked = keep.tile([P, S], U32, name="d_picked", tag="reused", align_bytes=64)
        d_codes = keep.tile([P, S], U32, name="d_codes", align_bytes=64)
        x_codes = keep.tile([P, S], U32, name="x_codes", align_bytes=64)
        nc.vector.tensor_copy(d_picked[:], d_word_table[:].indirect(k1_t[:]))
        nc.vector.tensor_copy(
            d_codes[:].bitcast(I32).rearrange("p (t m) -> p m t", t=PACK),
            d_picked[:].bitcast(I32).rearrange("p (m t) -> p m t", t=PACK),
        )

        def half(u):
            return slice(u * HALF, (u + 1) * HALF)

        def list_half(u):
            return slice(u * HALF // 16, (u + 1) * HALF // 16)

        for u in range(2):
            nc.vector.tensor_copy(x_codes[:, half(u)], x_word_table[:].indirect(offs_t[:, list_half(u)]))

        def first_product(t, lo, hi):
            cols = slice(t * P, (t + 1) * P)
            acc = psum.tile([P, S], F32, name="acc")
            nc.tensor.matmul_mx(
                out=acc[:, 0 : hi - lo],
                lhsT=d_codes[:, cols].bitcast(FP8X4),
                lhsT_scale=planes[:, cols],
                rhs=x_codes[:, lo:hi].bitcast(FP8X4),
                rhs_scale=planes[:, S + lo : S + hi],
                start=True,
                stop=True,
            )
            return acc[:, 0 : hi - lo]

        h0_halves = [first_product(0, u * HALF, (u + 1) * HALF) for u in range(2)]
        h_acc = {t: first_product(t, 0, S) for t in range(1, PACK)}

        nc.vector.tensor_copy(w_view[:, W_EARLY // PACK : P, :, :], w_late[:].rearrange("p j (m t) -> p m t j", t=PACK))
        w_codes = keep.tile([P, S], U32, name="w_codes", align_bytes=64)
        w_scales = keep.tile([P, S], U8, name="w_scales", align_bytes=64)
        nc.vector.quantize_mx(out=w_codes[:].bitcast(FP8X4), scales=w_scales[:], in_=w_bf[:])

        ex = [keep.tile([P, S], F32, name=f"ex{t}") for t in range(PACK)]
        em = [keep.tile([P, S], F32, name=f"em{t}") for t in range(PACK)]
        sums = [[keep.tile([P, HALF], F32, name=f"sum{t}_{u}") for u in range(2)] for t in range(PACK)]
        ratio = [keep.tile([P, PACK, HALF], F32, name=f"ratio{u}") for u in range(2)]
        LAST = PACK - 1
        other = [[keep.tile([P, HALF], F32, name=f"other{t}_{u}")[:] for u in range(2)] for t in range(LAST)]
        other.append([ratio[u][:, LAST - 1, :] for u in range(2)])

        def make_ex(t):
            nc.scalar.activation(ex[t][:], h_acc[t], ACT.Exp, scale=0.0625)

        def make_em(t):
            nc.scalar.activation(em[t][:], h_acc[t], ACT.Exp, scale=-0.0625)

        def make_other(t, u):
            if t == LAST:
                nc.scalar.activation(other[t][u], ex[t][:].indirect(n1_t[:, list_half(u)]), ACT.Copy)
            else:
                nc.scalar.activation(other[t][u], h_acc[t][:, half(u)], ACT.Exp, scale=0.0625)

        def add_partner(t, u):
            if t == LAST:
                nc.vector.tensor_tensor(sums[t][u][:], other[t][u], ex[t][:, half(u)], ALU.add)
            else:
                nc.vector.tensor_tensor(sums[t][u][:], ex[t][:].indirect(n1_t[:, list_half(u)]), other[t][u], ALU.add)

        def divide(t, u):
            nc.vector.tensor_tensor(ratio[u][:, t, :], em[t][:].indirect(n2_t[:, list_half(u)]), sums[t][u][:], ALU.mult)

        for u in range(2):
            nc.scalar.activation(ex[0][:, half(u)], h0_halves[u], ACT.Exp, scale=0.0625)
            nc.scalar.activation(other[0][u], h0_halves[u], ACT.Exp, scale=0.0625)
        for u in range(2):
            nc.scalar.activation(em[0][:, half(u)], h0_halves[u], ACT.Exp, scale=-0.0625)
        make_ex(1)
        for u in range(2):
            make_other(1, u)
        make_em(1)
        for t in (0, 1):
            for u in range(2):
                add_partner(t, u)
            for u in range(2):
                divide(t, u)
        for t in (2, 3):
            make_ex(t)
            make_other(t, 0)
        for t in (2, 3):
            make_em(t)
        for t in (2, 3):
            make_other(t, 1)
        for u in range(2):
            for t in (2, 3):
                add_partner(t, u)
            for t in (2, 3):
                divide(t, u)

        h2 = [keep.tile([P, S], F32, name=f"h2_{t}") for t in range(PACK)]
        h2_acc = {}
        z_codes = [keep.tile([P, HALF], U32, name=f"z_codes{u}", align_bytes=64) for u in range(2)]
        z_scales = [keep.tile([P, HALF], U8, name=f"z_scales{u}", align_bytes=64) for u in range(2)]
        z_bf = {}

        def make_z(u, lo, hi, tag):
            logs = keep.tile([P, (hi - lo) * PACK], F32, name=f"logs{u}_{lo}")
            nc.scalar.activation(
                logs[:].rearrange("p (c i t) -> p c t i", i=4, t=PACK),
                ratio[u][:, :, lo:hi].rearrange("p t (c i) -> p c t i", i=4),
                ACT.Ln,
            )
            zb = keep.tile([P, (hi - lo) * PACK], BF16, name=f"z_bf{u}_{lo}", tag=tag, align_bytes=64)
            nc.vector.tensor_tensor(
                zb[:].rearrange("p (j t) -> p j t", t=PACK),
                logs[:].rearrange("p (j t) -> p j t", t=PACK),
                gain[:].unsqueeze(1).to_broadcast([P, hi - lo, PACK]),
                ALU.mult,
            )
            z_bf[(u, lo)] = zb

        def quantise_z(u, lo, hi):
            nc.vector.quantize_mx(out=z_codes[u][:, lo:hi].bitcast(FP8X4), scales=z_scales[u][:, lo:hi], in_=z_bf[(u, lo)][:])

        def second_product(u):
            for t in range(PACK):
                cols = slice(t * P, (t + 1) * P)
                acc = psum.tile([P, S], F32, name="acc")
                nc.tensor.matmul_mx(
                    out=acc[:, 0:HALF],
                    lhsT=w_codes[:, cols].bitcast(FP8X4),
                    lhsT_scale=w_scales[:, cols],
                    rhs=z_codes[u][:].bitcast(FP8X4),
                    rhs_scale=z_scales[u][:],
                    start=True,
                    stop=True,
                )
                h2_acc[(t, u)] = acc

        Q = HALF // 2
        make_z(0, 0, HALF, "z_wide")
        make_z(1, 0, Q, "z_narrow")
        quantise_z(0, 0, HALF)
        second_product(0)
        make_z(1, Q, HALF, "z_wide")
        quantise_z(1, 0, Q)
        quantise_z(1, Q, HALF)
        second_product(1)
        for t in range(PACK):
            nc.scalar.copy(h2[t][:, half(0)], h2_acc[(t, 0)][:, 0:HALF])

        out_rows = out.rearrange("(p t) c -> t p c", t=PACK)
        for group in ((0,), (1,), (2, 3)):
            name = "_".join(str(t) for t in group)
            pa = keep.tile([P, len(group), PAIRS], F32, name="pa" + name)
            pb = keep.tile([P, len(group), PAIRS], F32, name="pb" + name)
            ra = keep.tile([P, len(group), PAIRS], F32, name="ra" + name)
            for i, t in enumerate(group):
                nc.scalar.copy(h2[t][:, half(1)], h2_acc[(t, 1)][:, 0:HALF])
                nc.scalar.activation(pa[:, i, :], h2[t][:].indirect(n3_t[:]), ACT.Copy)
                if t == 0:
                    nc.vector.tensor_copy(pb[:, i, :], h2[t][:].indirect(n4_t[:]))
                else:
                    nc.scalar.activation(pb[:, i, :], h2[t][:].indirect(n4_t[:]), ACT.Copy)
            nc.vector.tensor_tensor(ra[:], pa[:], pb[:], ALU.max)
            for i, t in enumerate(group):
                nc.vector.tensor_copy(h2[t][:].indirect(n3_t[:]), ra[:, i, :])
                nc.sync.dma_start(out_rows[t], h2[t][:])
